import numpy as np
import ml_dtypes


def mxq(x, axis, fmt="e4m3"):
    dtype, down = {"e4m3": (ml_dtypes.float8_e4m3fn, 7), "e5m2": (ml_dtypes.float8_e5m2, 14)}[fmt]
    v = np.moveaxis(np.asarray(x, np.float32).astype(ml_dtypes.bfloat16).astype(np.float64), axis, -1)
    blocks = v.reshape(v.shape[:-1] + (-1, 32))
    amax = np.abs(blocks).max(-1, keepdims=True)
    byte = np.maximum(np.where(amax > 0, np.frexp(amax)[1] - 1 + 127, 0) - down, 1)
    scale = np.exp2(byte - 127.0)
    codes = (blocks / scale).astype(np.float32).astype(dtype).astype(np.float64)
    return np.moveaxis((codes * scale).reshape(v.shape), -1, axis)


WIDE = False


def mx_kscale(k):
    if not WIDE:
        return np.ones(k)
    levels = np.array([10, -10, 5, -5, 0])
    if k % 512:
        return np.exp2(np.random.permutation(np.resize(levels, k // 32))).repeat(32)
    a = np.empty((k // 512, 16))
    for p in range(k // 512):
        a[p, :8] = np.random.permutation(np.resize(levels, 8))
        for g in range(8):
            far = levels[np.abs(levels - a[p, g]) >= 10]
            a[p, g + 8] = far[np.random.randint(len(far))]
    return np.exp2(a.ravel()).repeat(32)


def f64(x):
    return np.asarray(x).astype(np.float64)


def striped(idx):
    return np.tile(np.asarray(idx).reshape(-1, 16).T, (8, 1)).astype(np.uint16)


def unstriped(offs):
    return offs[:16].T.reshape(-1).astype(np.int64)


E2M1 = np.array([0.0, 0.5, 1.0, 1.5, 2.0, 3.0, 4.0, 6.0, -0.0, -0.5, -1.0, -1.5, -2.0, -3.0, -4.0, -6.0])


def pack_weight(w, fmt):
    k, n = w.shape
    w = f64(np.asarray(w, np.float32).astype(ml_dtypes.bfloat16)).reshape(k // 32, 32, n)
    amax = np.abs(w).max(1)
    if fmt == "e4m3":
        byte = np.frexp(amax)[1] - 1 + 127 - 7
    else:
        mant, ex = np.frexp(amax / 6.0)
        byte = np.where(mant > 0.5, ex, ex - 1) + 127
    byte = np.clip(np.where(amax > 0, byte, 1), 1, 254)
    scaled = (w * np.exp2(127.0 - byte)[:, None, :]).reshape(k, n).astype(np.float32)
    by_word = np.ascontiguousarray(scaled.reshape(k // 512, 128, 4, n).transpose(0, 1, 3, 2))
    if fmt == "e4m3":
        words = by_word.astype(ml_dtypes.float8_e4m3fn).view(np.uint8)
    else:
        c = by_word.astype(ml_dtypes.float4_e2m1fn).view(np.uint8) & 0xF
        words = (c[..., 0::2] | (c[..., 1::2] << 4)).reshape(k // 512, 128, 2 * n)
    return np.ascontiguousarray(words), np.ascontiguousarray(byte.astype(np.uint8).reshape(k // 512, 16, n))


def unpack_weight(words, scales, fmt):
    g, _, n = scales.shape
    words = np.ascontiguousarray(words).reshape(g, 128, n, -1)
    if fmt == "e4m3":
        vals = words.view(ml_dtypes.float8_e4m3fn).astype(np.float64)
    else:
        nib = np.empty((g, 128, n, 4), np.uint8)
        nib[..., 0::2] = words & 0xF
        nib[..., 1::2] = words >> 4
        vals = E2M1[nib]
    vals = vals * np.repeat(np.exp2(scales.astype(np.float64) - 127.0), 8, axis=1)[..., None]
    return vals.transpose(0, 1, 3, 2).reshape(g * 512, n)


B, N, T, D, NQ = 1, 512, 2048, 1024, 128
SEG = 16


def setup_inputs():
    n = np.random.standard_normal
    pages = np.random.permutation(T // 16)[:B * N // 16]
    idx = (pages[:, None] * 16 + np.arange(16)[None, :]).reshape(-1)
    s = mx_kscale(D)[:, None]
    kp = pack_weight(n((D, T)) / s, "e2m1")
    cp = pack_weight(n((D, T)) / s / 12, "e2m1")
    return {
        "qT": (n((B, D, NQ)) * s * (1.00 / np.sqrt(D))).astype(np.float32),
        "k_words": np.ascontiguousarray(kp[0].reshape(1, 2, 128, T, 2).transpose(0, 2, 3, 1, 4)).reshape(1, 128, T, 4),
        "k_scales": kp[1],
        "c_words": np.ascontiguousarray(cp[0].reshape(1, 2, 128, T, 2).transpose(0, 2, 3, 1, 4)).reshape(1, 128, T, 4),
        "c_scales": cp[1],
        "offs": striped(idx),
    }


def reference(qT, k_words, k_scales, c_words, c_scales, offs):
    idx = unstriped(offs)
    pick = lambda x, which: x[:, which].reshape(x.shape[0], B, -1).transpose(1, 0, 2)
    k = unpack_weight(k_words.reshape(1, 128, T, 2, 2).transpose(0, 3, 1, 2, 4).reshape(2, 128, 2 * T), k_scales, "e2m1")
    kg = pick(k, idx)
    c = unpack_weight(c_words.reshape(1, 128, T, 2, 2).transpose(0, 3, 1, 2, 4).reshape(2, 128, 2 * T), c_scales, "e2m1")
    cg = pick(c, idx)
    qq = mxq(f64(qT), 1, "e4m3")
    a = (qq.transpose(0, 2, 1) @ kg) + (qq.transpose(0, 2, 1) @ cg)
    y = a.reshape(B, NQ, N // SEG, SEG).max(-1)
    return y

@@ -1,0 +1,117 @@
+from contextlib import ExitStack
+
+import concourse.mybir as mybir
+
+F32 = mybir.dt.float32
+BF16 = mybir.dt.bfloat16
+I32 = mybir.dt.int32
+U32 = mybir.dt.uint32
+U16 = mybir.dt.uint16
+U8 = mybir.dt.uint8
+FP8X4 = mybir.dt.float8_e4m3fn_x4
+FP4X4 = mybir.dt.float4_e2m1fn_x4
+
+P = 128
+PACK = 4
+PASSES = 2
+TOKENS = 2048
+SLOTS = 512
+QUERIES = 128
+SEG = 16
+FLOPS = 2 * 2 * QUERIES * SLOTS * PASSES * P * PACK
+
+
+def tile_attend_residseg_kernel(tc, qT, k_words, k_scales, c_words, c_scales, offs, out):
+    nc = tc.nc
+    with ExitStack() as ctx:
+        keep = ctx.enter_context(tc.tile_pool(name="keep", bufs=1))
+        psum = ctx.enter_context(tc.psum_pool(name="psum", bufs=1))
+
+        offsets = keep.tile([P, SLOTS // 16], U16, name="offsets")
+        nc.sync.dma_start(offsets[:], offs)
+
+        word_pools = []
+        for name, words in (("k", k_words), ("c", c_words)):
+            word_pools.append(keep.tile([P, TOKENS], I32, name=name + "_word_pool", align_bytes=64))
+        q_raw = keep.tile([P, PASSES, PACK, QUERIES], F32, name="q_raw", align_bytes=64)
+
+        def load_words(level, words):
+            nc.sync.dma_start(word_pools[level][:], words[0].rearrange("p t b -> p (t b)").bitcast(I32))
+
+        load_words(0, k_words)
+
+        scale_pools = []
+        for name, scales in (("k", k_scales), ("c", c_scales)):
+            pool_tile = keep.tile([P, TOKENS // 4], I32, name=name + "_scale_pool", align_bytes=64)
+            nc.vector.memset(pool_tile[:], 0)
+            nc.scalar.dma_start(pool_tile[0:P:4, :], scales.bitcast(I32).rearrange("o f t -> f o t"))
+            scale_pools.append(pool_tile)
+
+        nc.sync.dma_start(
+            q_raw[:].rearrange("p o j w -> p o (j w)"),
+            qT[0].rearrange("(o p j) w -> p o (j w)", o=PASSES, j=PACK),
+        )
+        load_words(1, c_words)
+
+        planes = keep.tile([P, PASSES, 2 * SLOTS // 4], I32, name="planes", align_bytes=64)
+        nc.vector.memset(planes[:], 0)
+
+        picked_scales = keep.tile([P, 2 * SLOTS], U8, name="picked_scales", align_bytes=64)
+        for level in range(2):
+            nc.vector.tensor_copy(
+                picked_scales[:, level * SLOTS : (level + 1) * SLOTS],
+                scale_pools[level][:].bitcast(U8).indirect(offsets[:]),
+            )
+        for quad in range(4):
+            nc.scalar.dma_start(
+                planes[32 * quad : 32 * quad + 4, :, :],
+                picked_scales[32 * quad : 32 * quad + 32 : 4, :].bitcast(I32),
+            )
+
+        parted = []
+
+        def pick_words(level, name):
+            picked = keep.tile([P, SLOTS], U32, name=name + "_picked", align_bytes=64)
+            nc.vector.tensor_copy(picked[:], word_pools[level][:].bitcast(U32).indirect(offsets[:]))
+            halves = picked[:].bitcast(U16).rearrange("p (n o) -> p o n", o=PASSES)
+            for o in range(PASSES):
+                one = keep.tile([P, 2 * SLOTS], U8, name="%s_pass%d" % (name, o), align_bytes=64)
+                nc.vector.tensor_copy(one[:].bitcast(U16), halves[:, o, :])
+                parted.append(one)
+
+        pick_words(0, "k")
+
+        q_bf = keep.tile([P, PASSES, QUERIES, PACK], BF16, name="q_bf", align_bytes=64)
+        nc.vector.tensor_copy(q_bf[:], q_raw[:].rearrange("p o j w -> p o w j"))
+        q_codes = keep.tile([P, PASSES * QUERIES], U32, name="q_codes", align_bytes=64)
+        q_scales = keep.tile([P, PASSES * QUERIES], U8, name="q_scales", align_bytes=64)
+        nc.vector.quantize_mx(
+            out=q_codes[:].bitcast(FP8X4),
+            scales=q_scales[:],
+            in_=q_bf[:].rearrange("p o w j -> p (o w j)"),
+        )
+
+        pick_words(1, "c")
+
+        scores = psum.tile([P, SLOTS], F32, name="scores")
+        for level in range(2):
+            for o in range(PASSES):
+                cols = slice(o * QUERIES, (o + 1) * QUERIES)
+                nc.tensor.matmul_mx(
+                    out=scores[:],
+                    lhsT=q_codes[:, cols].bitcast(FP8X4),
+                    lhsT_scale=q_scales[:, cols],
+                    rhs=parted[PASSES * level + o][:].bitcast(FP4X4),
+                    rhs_scale=planes[:, o, :].bitcast(U8)[:, level * SLOTS : (level + 1) * SLOTS],
+                    start=(level == 0 and o == 0),
+                    stop=(level == 1 and o == PASSES - 1),
+                )
+
+        best = keep.tile([P, SLOTS // SEG], F32, name="best")
+        nc.vector.tensor_reduce(
+            out=best[:],
+            in_=scores[:].rearrange("p (j s) -> p j s", s=SEG),
+            axis=mybir.AxisListType.X,
+            op=mybir.AluOpType.max,
+        )
+        nc.sync.dma_start(out[0], best[:])

@@ -18,6 +18,7 @@ TOKENS = 2048
 SLOTS = 512
 QUERIES = 128
 SEG = 16
+GROUP = 128
 FLOPS = 2 * 2 * QUERIES * SLOTS * PASSES * P * PACK
 
 
@@ -38,14 +39,14 @@ def tile_attend_residseg_kernel(tc, qT, k_words, k_scales, c_words, c_scales, of
         def load_words(level, words):
             nc.sync.dma_start(word_pools[level][:], words[0].rearrange("p t b -> p (t b)").bitcast(I32))
 
-        load_words(0, k_words)
-
         scale_pools = []
         for name, scales in (("k", k_scales), ("c", c_scales)):
             pool_tile = keep.tile([P, TOKENS // 4], I32, name=name + "_scale_pool", align_bytes=64)
-            nc.vector.memset(pool_tile[:], 0)
-            nc.scalar.dma_start(pool_tile[0:P:4, :], scales.bitcast(I32).rearrange("o f t -> f o t"))
+            nc.vector.memset(pool_tile[0:96, :], 0)
+            nc.sync.dma_start(pool_tile[96:P, :], scales.bitcast(I32).rearrange("o f t -> f o t"))
             scale_pools.append(pool_tile)
+
+        load_words(0, k_words)
 
         nc.sync.dma_start(
             q_raw[:].rearrange("p o j w -> p o (j w)"),
@@ -65,21 +66,26 @@ def tile_attend_residseg_kernel(tc, qT, k_words, k_scales, c_words, c_scales, of
         for quad in range(4):
             nc.scalar.dma_start(
                 planes[32 * quad : 32 * quad + 4, :, :],
-                picked_scales[32 * quad : 32 * quad + 32 : 4, :].bitcast(I32),
+                picked_scales[96 + 8 * quad : 96 + 8 * quad + 8, :].bitcast(I32),
             )
 
-        parted = []
+        def pick_words(level, name, first, count):
+            picked = keep.tile([P, count], U32, name=name + "_picked", align_bytes=64)
+            nc.vector.tensor_copy(
+                picked[:],
+                word_pools[level][:].bitcast(U32).indirect(offsets[:, first // 16 : (first + count) // 16]),
+            )
+            return picked
 
-        def pick_words(level, name):
-            picked = keep.tile([P, SLOTS], U32, name=name + "_picked", align_bytes=64)
-            nc.vector.tensor_copy(picked[:], word_pools[level][:].bitcast(U32).indirect(offsets[:]))
-            halves = picked[:].bitcast(U16).rearrange("p (n o) -> p o n", o=PASSES)
-            for o in range(PASSES):
-                one = keep.tile([P, 2 * SLOTS], U8, name="%s_pass%d" % (name, o), align_bytes=64)
-                nc.vector.tensor_copy(one[:].bitcast(U16), halves[:, o, :])
-                parted.append(one)
+        def part_words(picked, name, count):
+            parted = keep.tile([P, PASSES, 2 * count], U8, name=name + "_parted", align_bytes=64)
+            nc.vector.tensor_copy(
+                parted[:].bitcast(U16),
+                picked[:].bitcast(U16).rearrange("p (n o) -> p o n", o=PASSES),
+            )
+            return parted
 
-        pick_words(0, "k")
+        k_parted = part_words(pick_words(0, "k", 0, SLOTS), "k", SLOTS)
 
         q_bf = keep.tile([P, PASSES, QUERIES, PACK], BF16, name="q_bf", align_bytes=64)
         nc.vector.tensor_copy(q_bf[:], q_raw[:].rearrange("p o j w -> p o w j"))
@@ -91,27 +97,38 @@ def tile_attend_residseg_kernel(tc, qT, k_words, k_scales, c_words, c_scales, of
             in_=q_bf[:].rearrange("p o w j -> p (o w j)"),
         )
 
-        pick_words(1, "c")
+        half = SLOTS // 2
+        c_picked = [pick_words(1, "c%d" % h, h * half, half) for h in range(2)]
+        c_parted = [part_words(c_picked[h], "c%d" % h, half) for h in range(2)]
 
-        scores = psum.tile([P, SLOTS], F32, name="scores")
-        for level in range(2):
-            for o in range(PASSES):
-                cols = slice(o * QUERIES, (o + 1) * QUERIES)
-                nc.tensor.matmul_mx(
-                    out=scores[:],
-                    lhsT=q_codes[:, cols].bitcast(FP8X4),
-                    lhsT_scale=q_scales[:, cols],
-                    rhs=parted[PASSES * level + o][:].bitcast(FP4X4),
-                    rhs_scale=planes[:, o, :].bitcast(U8)[:, level * SLOTS : (level + 1) * SLOTS],
-                    start=(level == 0 and o == 0),
-                    stop=(level == 1 and o == PASSES - 1),
-                )
+        scores = [psum.tile([P, GROUP], F32, name="scores%d" % g) for g in range(SLOTS // GROUP)]
+
+        def multiply(level, o, g, parted, first):
+            cols = slice(o * QUERIES, (o + 1) * QUERIES)
+            at = level * SLOTS + g * GROUP
+            nc.tensor.matmul_mx(
+                out=scores[g][:],
+                lhsT=q_codes[:, cols].bitcast(FP8X4),
+                lhsT_scale=q_scales[:, cols],
+                rhs=parted[:, o, 2 * first : 2 * (first + GROUP)].bitcast(FP4X4),
+                rhs_scale=planes[:, o, :].bitcast(U8)[:, at : at + GROUP],
+                start=(level == 0 and o == 0),
+                stop=(level == 1 and o == PASSES - 1),
+            )
+
+        for o in range(PASSES):
+            for g in range(SLOTS // GROUP):
+                multiply(0, o, g, k_parted, g * GROUP)
 
         best = keep.tile([P, SLOTS // SEG], F32, name="best")
-        nc.vector.tensor_reduce(
-            out=best[:],
-            in_=scores[:].rearrange("p (j s) -> p j s", s=SEG),
-            axis=mybir.AxisListType.X,
-            op=mybir.AluOpType.max,
-        )
+        per_group = GROUP // SEG
+        for g in range(SLOTS // GROUP):
+            for o in range(PASSES):
+                multiply(1, o, g, c_parted[g * GROUP // half], g * GROUP % half)
+            nc.vector.tensor_reduce(
+                out=best[:, g * per_group : (g + 1) * per_group],
+                in_=scores[g][:].rearrange("p (j s) -> p j s", s=SEG),
+                axis=mybir.AxisListType.X,
+                op=mybir.AluOpType.max,
+            )
         nc.sync.dma_start(out[0], best[:])

@@ -32,42 +32,45 @@ def tile_attend_residseg_kernel(tc, qT, k_words, k_scales, c_words, c_scales, of
         nc.sync.dma_start(offsets[:], offs)
 
         word_pools = []
-        for name, words in (("k", k_words), ("c", c_words)):
-            word_pools.append(keep.tile([P, TOKENS], I32, name=name + "_word_pool", align_bytes=64))
         q_raw = keep.tile([P, PASSES, PACK, QUERIES], F32, name="q_raw", align_bytes=64)
 
-        def load_words(level, words):
-            nc.sync.dma_start(word_pools[level][:], words[0].rearrange("p t b -> p (t b)").bitcast(I32))
+        def load_words(name, words, tag):
+            pool_tile = keep.tile([P, TOKENS], I32, name=name + "_word_pool", tag=tag, align_bytes=64)
+            nc.sync.dma_start(pool_tile[:], words[0].rearrange("p t b -> p (t b)").bitcast(I32))
+            word_pools.append(pool_tile)
 
         scale_pools = []
         for name, scales in (("k", k_scales), ("c", c_scales)):
-            pool_tile = keep.tile([P, TOKENS // 4], I32, name=name + "_scale_pool", align_bytes=64)
+            pool_tile = keep.tile([P, TOKENS // 4], I32, name=name + "_scale_pool", tag=name + "_first", align_bytes=64)
             nc.vector.memset(pool_tile[0:96, :], 0)
             nc.sync.dma_start(pool_tile[96:P, :], scales.bitcast(I32).rearrange("o f t -> f o t"))
             scale_pools.append(pool_tile)
 
-        load_words(0, k_words)
+        load_words("k", k_words, "k_words")
 
         nc.sync.dma_start(
             q_raw[:].rearrange("p o j w -> p o (j w)"),
             qT[0].rearrange("(o p j) w -> p o (j w)", o=PASSES, j=PACK),
         )
-        load_words(1, c_words)
 
-        planes = keep.tile([P, PASSES, 2 * SLOTS // 4], I32, name="planes", align_bytes=64)
-        nc.vector.memset(planes[:], 0)
+        planes = []
+        for name in ("k", "c"):
+            plane = keep.tile([P, PASSES, SLOTS // 4], I32, name=name + "_planes", align_bytes=64)
+            nc.vector.memset(plane[:], 0)
+            planes.append(plane)
 
-        picked_scales = keep.tile([P, 2 * SLOTS], U8, name="picked_scales", align_bytes=64)
-        for level in range(2):
-            nc.vector.tensor_copy(
-                picked_scales[:, level * SLOTS : (level + 1) * SLOTS],
-                scale_pools[level][:].bitcast(U8).indirect(offsets[:]),
-            )
-        for quad in range(4):
-            nc.scalar.dma_start(
-                planes[32 * quad : 32 * quad + 4, :, :],
-                picked_scales[96 + 8 * quad : 96 + 8 * quad + 8, :].bitcast(I32),
-            )
+        def pick_scales(level, name, queues):
+            picked = keep.tile([P, SLOTS], U8, name=name + "_picked_scales", align_bytes=64)
+            nc.vector.tensor_copy(picked[:], scale_pools[level][:].bitcast(U8).indirect(offsets[:]))
+            for quad in range(4):
+                queues[quad % len(queues)].dma_start(
+                    planes[level][32 * quad : 32 * quad + 4, :, :],
+                    picked[96 + 8 * quad : 96 + 8 * quad + 8, :].bitcast(I32),
+                )
+
+        pick_scales(0, "k", [nc.sync, nc.scalar])
+        load_words("c", c_words, "k_first")
+        pick_scales(1, "c", [nc.sync])
 
         def pick_words(level, name, first, count):
             picked = keep.tile([P, count], U32, name=name + "_picked", align_bytes=64)
@@ -81,11 +84,11 @@ def tile_attend_residseg_kernel(tc, qT, k_words, k_scales, c_words, c_scales, of
             parted = keep.tile([P, PASSES, 2 * count], U8, name=name + "_parted", align_bytes=64)
             nc.vector.tensor_copy(
                 parted[:].bitcast(U16),
-                picked[:].bitcast(U16).rearrange("p (n o) -> p o n", o=PASSES),
+                picked.bitcast(U16).rearrange("p (n o) -> p o n", o=PASSES),
             )
             return parted
 
-        k_parted = part_words(pick_words(0, "k", 0, SLOTS), "k", SLOTS)
+        k_parted = part_words(pick_words(0, "k", 0, SLOTS)[:], "k", SLOTS)
 
         q_bf = keep.tile([P, PASSES, QUERIES, PACK], BF16, name="q_bf", align_bytes=64)
         nc.vector.tensor_copy(q_bf[:], q_raw[:].rearrange("p o j w -> p o w j"))
@@ -99,19 +102,22 @@ def tile_attend_residseg_kernel(tc, qT, k_words, k_scales, c_words, c_scales, of
 
         half = SLOTS // 2
         c_picked = [pick_words(1, "c%d" % h, h * half, half) for h in range(2)]
-        c_parted = [part_words(c_picked[h], "c%d" % h, half) for h in range(2)]
+        c_parted = [
+            part_words(c_picked[at // half][:, at % half : at % half + GROUP], "c%d" % at, GROUP)
+            for at in range(0, SLOTS, GROUP)
+        ]
 
         scores = [psum.tile([P, GROUP], F32, name="scores%d" % g) for g in range(SLOTS // GROUP)]
 
         def multiply(level, o, g, parted, first):
             cols = slice(o * QUERIES, (o + 1) * QUERIES)
-            at = level * SLOTS + g * GROUP
+            at = g * GROUP
             nc.tensor.matmul_mx(
                 out=scores[g][:],
                 lhsT=q_codes[:, cols].bitcast(FP8X4),
                 lhsT_scale=q_scales[:, cols],
                 rhs=parted[:, o, 2 * first : 2 * (first + GROUP)].bitcast(FP4X4),
-                rhs_scale=planes[:, o, :].bitcast(U8)[:, at : at + GROUP],
+                rhs_scale=planes[level][:, o, :].bitcast(U8)[:, at : at + GROUP],
                 start=(level == 0 and o == 0),
                 stop=(level == 1 and o == PASSES - 1),
             )
@@ -124,7 +130,7 @@ def tile_attend_residseg_kernel(tc, qT, k_words, k_scales, c_words, c_scales, of
         per_group = GROUP // SEG
         for g in range(SLOTS // GROUP):
             for o in range(PASSES):
-                multiply(1, o, g, c_parted[g * GROUP // half], g * GROUP % half)
+                multiply(1, o, g, c_parted[g], 0)
             nc.vector.tensor_reduce(
                 out=best[:, g * per_group : (g + 1) * per_group],
                 in_=scores[g][:].rearrange("p (j s) -> p j s", s=SEG),

@@ -31,6 +31,11 @@ def tile_attend_residseg_kernel(tc, qT, k_words, k_scales, c_words, c_scales, of
         offsets = keep.tile([P, SLOTS // 16], U16, name="offsets")
         nc.sync.dma_start(offsets[:], offs)
 
+        warm_in = keep.tile([P, 8], F32, name="warm_in")
+        warm_out = keep.tile([P, 8], BF16, name="warm_out")
+        nc.gpsimd.memset(warm_in[:], 0.0)
+        nc.scalar.copy(warm_out[:], warm_in[:])
+
         word_pools = []
         q_raw = keep.tile([P, PASSES, PACK, QUERIES], F32, name="q_raw", align_bytes=64)
 
@@ -40,10 +45,14 @@ def tile_attend_residseg_kernel(tc, qT, k_words, k_scales, c_words, c_scales, of
             word_pools.append(pool_tile)
 
         scale_pools = []
-        for name, scales in (("k", k_scales), ("c", c_scales)):
+        first_row = (96, 32)
+        empty_rows = (((0, 96),), ((0, 32), (64, P)))
+        for level, (name, scales) in enumerate((("k", k_scales), ("c", c_scales))):
             pool_tile = keep.tile([P, TOKENS // 4], I32, name=name + "_scale_pool", tag=name + "_first", align_bytes=64)
-            nc.vector.memset(pool_tile[0:96, :], 0)
-            nc.sync.dma_start(pool_tile[96:P, :], scales.bitcast(I32).rearrange("o f t -> f o t"))
+            for lo, hi in empty_rows[level]:
+                nc.vector.memset(pool_tile[lo:hi, :], 0)
+            at = first_row[level]
+            nc.sync.dma_start(pool_tile[at : at + 32, :], scales.bitcast(I32).rearrange("o f t -> f o t"))
             scale_pools.append(pool_tile)
 
         load_words("k", k_words, "k_words")
@@ -56,7 +65,7 @@ def tile_attend_residseg_kernel(tc, qT, k_words, k_scales, c_words, c_scales, of
         planes = []
         for name in ("k", "c"):
             plane = keep.tile([P, PASSES, SLOTS // 4], I32, name=name + "_planes", align_bytes=64)
-            nc.vector.memset(plane[:], 0)
+            nc.gpsimd.memset(plane[:], 0)
             planes.append(plane)
 
         def pick_scales(level, name, queues):
@@ -65,10 +74,10 @@ def tile_attend_residseg_kernel(tc, qT, k_words, k_scales, c_words, c_scales, of
             for quad in range(4):
                 queues[quad % len(queues)].dma_start(
                     planes[level][32 * quad : 32 * quad + 4, :, :],
-                    picked[96 + 8 * quad : 96 + 8 * quad + 8, :].bitcast(I32),
+                    picked[first_row[level] + 8 * quad : first_row[level] + 8 * quad + 8, :].bitcast(I32),
                 )
 
-        pick_scales(0, "k", [nc.sync, nc.scalar])
+        pick_scales(0, "k", [nc.sync, nc.scalar, nc.scalar, nc.scalar])
         load_words("c", c_words, "k_first")
         pick_scales(1, "c", [nc.sync])
 
@@ -90,15 +99,19 @@ def tile_attend_residseg_kernel(tc, qT, k_words, k_scales, c_words, c_scales, of
 
         k_parted = part_words(pick_words(0, "k", 0, SLOTS)[:], "k", SLOTS)
 
-        q_bf = keep.tile([P, PASSES, QUERIES, PACK], BF16, name="q_bf", align_bytes=64)
-        nc.vector.tensor_copy(q_bf[:], q_raw[:].rearrange("p o j w -> p o w j"))
-        q_codes = keep.tile([P, PASSES * QUERIES], U32, name="q_codes", align_bytes=64)
-        q_scales = keep.tile([P, PASSES * QUERIES], U8, name="q_scales", align_bytes=64)
-        nc.vector.quantize_mx(
-            out=q_codes[:].bitcast(FP8X4),
-            scales=q_scales[:],
-            in_=q_bf[:].rearrange("p o w j -> p (o w j)"),
-        )
+        q_codes = []
+        q_scales = []
+        for o in range(PASSES):
+            rounded = keep.tile([P, QUERIES * PACK], BF16, name="q_bf%d" % o, align_bytes=64)
+            nc.scalar.copy(
+                rounded[:].rearrange("p (c i j) -> p c j i", i=4, j=PACK),
+                q_raw[:, o].rearrange("p j (c i) -> p c j i", i=4),
+            )
+            codes = keep.tile([P, QUERIES], U32, name="q_codes%d" % o, align_bytes=64)
+            scales = keep.tile([P, QUERIES], U8, name="q_scales%d" % o, align_bytes=64)
+            nc.vector.quantize_mx(out=codes[:].bitcast(FP8X4), scales=scales[:], in_=rounded[:])
+            q_codes.append(codes)
+            q_scales.append(scales)
 
         half = SLOTS // 2
         c_picked = [pick_words(1, "c%d" % h, h * half, half) for h in range(2)]
@@ -110,12 +123,11 @@ def tile_attend_residseg_kernel(tc, qT, k_words, k_scales, c_words, c_scales, of
         scores = [psum.tile([P, GROUP], F32, name="scores%d" % g) for g in range(SLOTS // GROUP)]
 
         def multiply(level, o, g, parted, first):
-            cols = slice(o * QUERIES, (o + 1) * QUERIES)
             at = g * GROUP
             nc.tensor.matmul_mx(
                 out=scores[g][:],
-                lhsT=q_codes[:, cols].bitcast(FP8X4),
-                lhsT_scale=q_scales[:, cols],
+                lhsT=q_codes[o][:].bitcast(FP8X4),
+                lhsT_scale=q_scales[o][:],
                 rhs=parted[:, o, 2 * first : 2 * (first + GROUP)].bitcast(FP4X4),
                 rhs_scale=planes[level][:, o, :].bitcast(U8)[:, at : at + GROUP],
                 start=(level == 0 and o == 0),
@@ -125,6 +137,17 @@ def tile_attend_residseg_kernel(tc, qT, k_words, k_scales, c_words, c_scales, of
         for o in range(PASSES):
             for g in range(SLOTS // GROUP):
                 multiply(0, o, g, k_parted, g * GROUP)
+
+        spare = psum.tile([P, SLOTS], F32, name="spare")
+        nc.tensor.matmul_mx(
+            out=spare[:],
+            lhsT=q_codes[1][:].bitcast(FP8X4),
+            lhsT_scale=q_scales[1][:],
+            rhs=k_parted[:, 1, :].bitcast(FP4X4),
+            rhs_scale=planes[0][:, 1, :].bitcast(U8),
+            start=True,
+            stop=True,
+        )
 
         best = keep.tile([P, SLOTS // SEG], F32, name="best")
         per_group = GROUP // SEG

@@ -33,7 +33,7 @@ def tile_attend_residseg_kernel(tc, qT, k_words, k_scales, c_words, c_scales, of
 
         warm_in = keep.tile([P, 8], F32, name="warm_in")
         warm_out = keep.tile([P, 8], BF16, name="warm_out")
-        nc.gpsimd.memset(warm_in[:], 0.0)
+        nc.vector.memset(warm_in[:], 0.0)
         nc.scalar.copy(warm_out[:], warm_in[:])
 
         word_pools = []
@@ -65,7 +65,7 @@ def tile_attend_residseg_kernel(tc, qT, k_words, k_scales, c_words, c_scales, of
         planes = []
         for name in ("k", "c"):
             plane = keep.tile([P, PASSES, SLOTS // 4], I32, name=name + "_planes", align_bytes=64)
-            nc.gpsimd.memset(plane[:], 0)
+            nc.vector.memset(plane[:], 0)
             planes.append(plane)
 
         def pick_scales(level, name, queues):
@@ -77,17 +77,15 @@ def tile_attend_residseg_kernel(tc, qT, k_words, k_scales, c_words, c_scales, of
                     picked[first_row[level] + 8 * quad : first_row[level] + 8 * quad + 8, :].bitcast(I32),
                 )
 
-        pick_scales(0, "k", [nc.sync, nc.scalar, nc.scalar, nc.scalar])
+        pick_scales(0, "k", [nc.sync, nc.scalar])
         load_words("c", c_words, "k_first")
         pick_scales(1, "c", [nc.sync])
 
-        def pick_words(level, name, first, count):
-            picked = keep.tile([P, count], U32, name=name + "_picked", align_bytes=64)
+        def pick_words(level, picked, first, count):
             nc.vector.tensor_copy(
-                picked[:],
+                picked[:, first : first + count],
                 word_pools[level][:].bitcast(U32).indirect(offsets[:, first // 16 : (first + count) // 16]),
             )
-            return picked
 
         def part_words(picked, name, count):
             parted = keep.tile([P, PASSES, 2 * count], U8, name=name + "_parted", align_bytes=64)
@@ -97,26 +95,31 @@ def tile_attend_residseg_kernel(tc, qT, k_words, k_scales, c_words, c_scales, of
             )
             return parted
 
-        k_parted = part_words(pick_words(0, "k", 0, SLOTS)[:], "k", SLOTS)
+        k_picked = keep.tile([P, SLOTS], U32, name="k_picked", align_bytes=64)
+        pick_words(0, k_picked, 0, SLOTS)
+        k_parted = part_words(k_picked[:], "k", SLOTS)
 
+        rounded = keep.tile([P, PASSES * QUERIES * PACK], BF16, name="q_bf", tag="staged", align_bytes=64)
         q_codes = []
         q_scales = []
         for o in range(PASSES):
-            rounded = keep.tile([P, QUERIES * PACK], BF16, name="q_bf%d" % o, align_bytes=64)
+            part = rounded[:, o * QUERIES * PACK : (o + 1) * QUERIES * PACK]
             nc.scalar.copy(
-                rounded[:].rearrange("p (c i j) -> p c j i", i=4, j=PACK),
+                part.rearrange("p (c i j) -> p c j i", i=4, j=PACK),
                 q_raw[:, o].rearrange("p j (c i) -> p c j i", i=4),
             )
             codes = keep.tile([P, QUERIES], U32, name="q_codes%d" % o, align_bytes=64)
             scales = keep.tile([P, QUERIES], U8, name="q_scales%d" % o, align_bytes=64)
-            nc.vector.quantize_mx(out=codes[:].bitcast(FP8X4), scales=scales[:], in_=rounded[:])
+            nc.vector.quantize_mx(out=codes[:].bitcast(FP8X4), scales=scales[:], in_=part)
             q_codes.append(codes)
             q_scales.append(scales)
 
         half = SLOTS // 2
-        c_picked = [pick_words(1, "c%d" % h, h * half, half) for h in range(2)]
+        c_picked = keep.tile([P, SLOTS], U32, name="c_picked", tag="staged", align_bytes=64)
+        for h in range(2):
+            pick_words(1, c_picked, h * half, half)
         c_parted = [
-            part_words(c_picked[at // half][:, at % half : at % half + GROUP], "c%d" % at, GROUP)
+            part_words(c_picked[:, at : at + GROUP], "c%d" % at, GROUP)
             for at in range(0, SLOTS, GROUP)
         ]
 

@@ -45,8 +45,8 @@ def tile_attend_residseg_kernel(tc, qT, k_words, k_scales, c_words, c_scales, of
             word_pools.append(pool_tile)
 
         scale_pools = []
-        first_row = (96, 32)
-        empty_rows = (((0, 96),), ((0, 32), (64, P)))
+        first_row = (96, 96)
+        empty_rows = (((0, 96),), ((0, 96),))
         for level, (name, scales) in enumerate((("k", k_scales), ("c", c_scales))):
             pool_tile = keep.tile([P, TOKENS // 4], I32, name=name + "_scale_pool", tag=name + "_first", align_bytes=64)
             for lo, hi in empty_rows[level]:
@@ -81,11 +81,13 @@ def tile_attend_residseg_kernel(tc, qT, k_words, k_scales, c_words, c_scales, of
         load_words("c", c_words, "k_first")
         pick_scales(1, "c", [nc.sync])
 
-        def pick_words(level, picked, first, count):
+        def pick_words(level, name, first, count):
+            picked = keep.tile([P, count], U32, name=name + "_picked", align_bytes=64)
             nc.vector.tensor_copy(
-                picked[:, first : first + count],
+                picked[:],
                 word_pools[level][:].bitcast(U32).indirect(offsets[:, first // 16 : (first + count) // 16]),
             )
+            return picked
 
         def part_words(picked, name, count):
             parted = keep.tile([P, PASSES, 2 * count], U8, name=name + "_parted", align_bytes=64)
@@ -95,31 +97,26 @@ def tile_attend_residseg_kernel(tc, qT, k_words, k_scales, c_words, c_scales, of
             )
             return parted
 
-        k_picked = keep.tile([P, SLOTS], U32, name="k_picked", align_bytes=64)
-        pick_words(0, k_picked, 0, SLOTS)
-        k_parted = part_words(k_picked[:], "k", SLOTS)
+        k_parted = part_words(pick_words(0, "k", 0, SLOTS)[:], "k", SLOTS)
 
-        rounded = keep.tile([P, PASSES * QUERIES * PACK], BF16, name="q_bf", tag="staged", align_bytes=64)
         q_codes = []
         q_scales = []
         for o in range(PASSES):
-            part = rounded[:, o * QUERIES * PACK : (o + 1) * QUERIES * PACK]
+            rounded = keep.tile([P, QUERIES * PACK], BF16, name="q_bf%d" % o, align_bytes=64)
             nc.scalar.copy(
-                part.rearrange("p (c i j) -> p c j i", i=4, j=PACK),
+                rounded[:].rearrange("p (c i j) -> p c j i", i=4, j=PACK),
                 q_raw[:, o].rearrange("p j (c i) -> p c j i", i=4),
             )
             codes = keep.tile([P, QUERIES], U32, name="q_codes%d" % o, align_bytes=64)
             scales = keep.tile([P, QUERIES], U8, name="q_scales%d" % o, align_bytes=64)
-            nc.vector.quantize_mx(out=codes[:].bitcast(FP8X4), scales=scales[:], in_=part)
+            nc.vector.quantize_mx(out=codes[:].bitcast(FP8X4), scales=scales[:], in_=rounded[:])
             q_codes.append(codes)
             q_scales.append(scales)
 
         half = SLOTS // 2
-        c_picked = keep.tile([P, SLOTS], U32, name="c_picked", tag="staged", align_bytes=64)
-        for h in range(2):
-            pick_words(1, c_picked, h * half, half)
+        c_picked = [pick_words(1, "c%d" % h, h * half, half) for h in range(2)]
         c_parted = [
-            part_words(c_picked[:, at : at + GROUP], "c%d" % at, GROUP)
+            part_words(c_picked[at // half][:, at % half : at % half + GROUP], "c%d" % at, GROUP)
             for at in range(0, SLOTS, GROUP)
         ]
 

@@ -160,4 +160,6 @@ def tile_attend_residseg_kernel(tc, qT, k_words, k_scales, c_words, c_scales, of
                 axis=mybir.AxisListType.X,
                 op=mybir.AluOpType.max,
             )
-        nc.sync.dma_start(out[0], best[:])
+            if g % 2 == 1:
+                done = slice((g - 1) * per_group, (g + 1) * per_group)
+                nc.sync.dma_start(out[0][:, done], best[:, done])

@@ -122,7 +122,7 @@ def tile_attend_residseg_kernel(tc, qT, k_words, k_scales, c_words, c_scales, of
 
         scores = [psum.tile([P, GROUP], F32, name="scores%d" % g) for g in range(SLOTS // GROUP)]
 
-        def multiply(level, o, g, parted, first):
+        def multiply(level, o, g, parted, first, last):
             at = g * GROUP
             nc.tensor.matmul_mx(
                 out=scores[g][:],
@@ -131,12 +131,12 @@ def tile_attend_residseg_kernel(tc, qT, k_words, k_scales, c_words, c_scales, of
                 rhs=parted[:, o, 2 * first : 2 * (first + GROUP)].bitcast(FP4X4),
                 rhs_scale=planes[level][:, o, :].bitcast(U8)[:, at : at + GROUP],
                 start=(level == 0 and o == 0),
-                stop=(level == 1 and o == PASSES - 1),
+                stop=last,
             )
 
         for o in range(PASSES):
             for g in range(SLOTS // GROUP):
-                multiply(0, o, g, k_parted, g * GROUP)
+                multiply(0, o, g, k_parted, g * GROUP, False)
 
         spare = psum.tile([P, SLOTS], F32, name="spare")
         nc.tensor.matmul_mx(
@@ -152,8 +152,9 @@ def tile_attend_residseg_kernel(tc, qT, k_words, k_scales, c_words, c_scales, of
         best = keep.tile([P, SLOTS // SEG], F32, name="best")
         per_group = GROUP // SEG
         for g in range(SLOTS // GROUP):
-            for o in range(PASSES):
-                multiply(1, o, g, c_parted[g], 0)
+            order = (1, 0) if g % 2 == 0 else (0, 1)
+            for o in order:
+                multiply(1, o, g, c_parted[g], 0, o == order[-1])
             nc.vector.tensor_reduce(
                 out=best[:, g * per_group : (g + 1) * per_group],
                 in_=scores[g][:].rearrange("p (j s) -> p j s", s=SEG),

@@ -31,11 +31,6 @@ def tile_attend_residseg_kernel(tc, qT, k_words, k_scales, c_words, c_scales, of
         offsets = keep.tile([P, SLOTS // 16], U16, name="offsets")
         nc.sync.dma_start(offsets[:], offs)
 
-        warm_in = keep.tile([P, 8], F32, name="warm_in")
-        warm_out = keep.tile([P, 8], BF16, name="warm_out")
-        nc.vector.memset(warm_in[:], 0.0)
-        nc.scalar.copy(warm_out[:], warm_in[:])
-
         word_pools = []
         q_raw = keep.tile([P, PASSES, PACK, QUERIES], F32, name="q_raw", align_bytes=64)
 
@@ -103,7 +98,7 @@ def tile_attend_residseg_kernel(tc, qT, k_words, k_scales, c_words, c_scales, of
         q_scales = []
         for o in range(PASSES):
             rounded = keep.tile([P, QUERIES * PACK], BF16, name="q_bf%d" % o, align_bytes=64)
-            nc.scalar.copy(
+            (nc.vector.tensor_copy, nc.scalar.copy)[o](
                 rounded[:].rearrange("p (c i j) -> p c j i", i=4, j=PACK),
                 q_raw[:, o].rearrange("p j (c i) -> p c j i", i=4),
             )

@@ -50,12 +50,11 @@ def tile_attend_residseg_kernel(tc, qT, k_words, k_scales, c_words, c_scales, of
             nc.sync.dma_start(pool_tile[at : at + 32, :], scales.bitcast(I32).rearrange("o f t -> f o t"))
             scale_pools.append(pool_tile)
 
-        load_words("k", k_words, "k_words")
-
         nc.sync.dma_start(
             q_raw[:].rearrange("p o j w -> p o (j w)"),
             qT[0].rearrange("(o p j) w -> p o (j w)", o=PASSES, j=PACK),
         )
+        load_words("k", k_words, "k_words")
 
         planes = []
         for name in ("k", "c"):
@@ -92,13 +91,11 @@ def tile_attend_residseg_kernel(tc, qT, k_words, k_scales, c_words, c_scales, of
             )
             return parted
 
-        k_parted = part_words(pick_words(0, "k", 0, SLOTS)[:], "k", SLOTS)
-
         q_codes = []
         q_scales = []
         for o in range(PASSES):
             rounded = keep.tile([P, QUERIES * PACK], BF16, name="q_bf%d" % o, align_bytes=64)
-            (nc.vector.tensor_copy, nc.scalar.copy)[o](
+            nc.vector.tensor_copy(
                 rounded[:].rearrange("p (c i j) -> p c j i", i=4, j=PACK),
                 q_raw[:, o].rearrange("p j (c i) -> p c j i", i=4),
             )
@@ -109,36 +106,43 @@ def tile_attend_residseg_kernel(tc, qT, k_words, k_scales, c_words, c_scales, of
             q_scales.append(scales)
 
         half = SLOTS // 2
-        c_picked = [pick_words(1, "c%d" % h, h * half, half) for h in range(2)]
-        c_parted = [
-            part_words(c_picked[at // half][:, at % half : at % half + GROUP], "c%d" % at, GROUP)
-            for at in range(0, SLOTS, GROUP)
-        ]
+        picked_words = []
+        parted_words = []
+        for level, name in enumerate(("k", "c")):
+            halves = [pick_words(level, "%s%d" % (name, h), h * half, half) for h in range(2)]
+            picked_words.append(halves)
+            parted_words.append(
+                [
+                    part_words(halves[at // half][:, at % half : at % half + GROUP], "%s%d" % (name, at), GROUP)
+                    for at in range(0, SLOTS, GROUP)
+                ]
+            )
 
         scores = [psum.tile([P, GROUP], F32, name="scores%d" % g) for g in range(SLOTS // GROUP)]
 
-        def multiply(level, o, g, parted, first, last):
+        def multiply(level, o, g, first, last):
             at = g * GROUP
             nc.tensor.matmul_mx(
                 out=scores[g][:],
                 lhsT=q_codes[o][:].bitcast(FP8X4),
                 lhsT_scale=q_scales[o][:],
-                rhs=parted[:, o, 2 * first : 2 * (first + GROUP)].bitcast(FP4X4),
+                rhs=parted_words[level][g][:, o, :].bitcast(FP4X4),
                 rhs_scale=planes[level][:, o, :].bitcast(U8)[:, at : at + GROUP],
-                start=(level == 0 and o == 0),
+                start=first,
                 stop=last,
             )
 
-        for o in range(PASSES):
-            for g in range(SLOTS // GROUP):
-                multiply(0, o, g, k_parted, g * GROUP, False)
+        for g in range(SLOTS // GROUP):
+            order = (1, 0) if g % 2 == 0 else (0, 1)
+            for o in order:
+                multiply(0, o, g, o == order[0], False)
 
         spare = psum.tile([P, SLOTS], F32, name="spare")
         nc.tensor.matmul_mx(
             out=spare[:],
             lhsT=q_codes[1][:].bitcast(FP8X4),
             lhsT_scale=q_scales[1][:],
-            rhs=k_parted[:, 1, :].bitcast(FP4X4),
+            rhs=picked_words[0][1][:].bitcast(U8).bitcast(FP4X4),
             rhs_scale=planes[0][:, 1, :].bitcast(U8),
             start=True,
             stop=True,
@@ -149,7 +153,7 @@ def tile_attend_residseg_kernel(tc, qT, k_words, k_scales, c_words, c_scales, of
         for g in range(SLOTS // GROUP):
             order = (1, 0) if g % 2 == 0 else (0, 1)
             for o in order:
-                multiply(1, o, g, c_parted[g], 0, o == order[-1])
+                multiply(1, o, g, False, o == order[-1])
             nc.vector.tensor_reduce(
                 out=best[:, g * per_group : (g + 1) * per_group],
                 in_=scores[g][:].rearrange("p (j s) -> p j s", s=SEG),

@@ -160,6 +160,6 @@ def tile_attend_residseg_kernel(tc, qT, k_words, k_scales, c_words, c_scales, of
                 axis=mybir.AxisListType.X,
                 op=mybir.AluOpType.max,
             )
-            if g % 2 == 1:
-                done = slice((g - 1) * per_group, (g + 1) * per_group)
+            if g in (0, SLOTS // GROUP - 1):
+                done = slice(min(g, 1) * per_group, (g + 1) * per_group)
                 nc.sync.dma_start(out[0][:, done], best[:, done])

@@ -83,12 +83,14 @@ def tile_attend_residseg_kernel(tc, qT, k_words, k_scales, c_words, c_scales, of
             )
             return picked
 
-        def part_words(picked, name, count):
+        def part_words(picked, name, count, order):
             parted = keep.tile([P, PASSES, 2 * count], U8, name=name + "_parted", align_bytes=64)
-            nc.vector.tensor_copy(
-                parted[:].bitcast(U16),
-                picked.bitcast(U16).rearrange("p (n o) -> p o n", o=PASSES),
-            )
+            halves = picked.bitcast(U16).rearrange("p (n o) -> p o n", o=PASSES)
+            if order is None:
+                nc.vector.tensor_copy(parted[:].bitcast(U16), halves)
+            else:
+                for o in order:
+                    nc.vector.tensor_copy(parted[:, o, :].bitcast(U16), halves[:, o, :])
             return parted
 
         q_codes = []
@@ -106,6 +108,7 @@ def tile_attend_residseg_kernel(tc, qT, k_words, k_scales, c_words, c_scales, of
             q_scales.append(scales)
 
         half = SLOTS // 2
+        by_pass = {(1, 0): (1, 0), (1, SLOTS - GROUP): (0, 1)}
         picked_words = []
         parted_words = []
         for level, name in enumerate(("k", "c")):
@@ -113,7 +116,7 @@ def tile_attend_residseg_kernel(tc, qT, k_words, k_scales, c_words, c_scales, of
             picked_words.append(halves)
             parted_words.append(
                 [
-                    part_words(halves[at // half][:, at % half : at % half + GROUP], "%s%d" % (name, at), GROUP)
+                    part_words(halves[at // half][:, at % half : at % half + GROUP], "%s%d" % (name, at), GROUP, by_pass.get((level, at)))
                     for at in range(0, SLOTS, GROUP)
                 ]
             )

@@ -19,6 +19,8 @@ SLOTS = 512
 QUERIES = 128
 SEG = 16
 GROUP = 128
+GROUPS = SLOTS // GROUP
+SCALE_ROW = 96
 FLOPS = 2 * 2 * QUERIES * SLOTS * PASSES * P * PACK
 
 
@@ -31,67 +33,40 @@ def tile_attend_residseg_kernel(tc, qT, k_words, k_scales, c_words, c_scales, of
         offsets = keep.tile([P, SLOTS // 16], U16, name="offsets")
         nc.sync.dma_start(offsets[:], offs)
 
-        word_pools = []
-        q_raw = keep.tile([P, PASSES, PACK, QUERIES], F32, name="q_raw", align_bytes=64)
+        def load_scales(name, scales):
+            pool_tile = keep.tile([P, TOKENS // 4], I32, name=name + "_scale_pool", tag=name + "_first", align_bytes=64)
+            nc.vector.memset(pool_tile[0:SCALE_ROW, :], 0)
+            nc.sync.dma_start(pool_tile[SCALE_ROW:P, :], scales.bitcast(I32).rearrange("o f t -> f o t"))
+            return pool_tile
 
         def load_words(name, words, tag):
             pool_tile = keep.tile([P, TOKENS], I32, name=name + "_word_pool", tag=tag, align_bytes=64)
             nc.sync.dma_start(pool_tile[:], words[0].rearrange("p t b -> p (t b)").bitcast(I32))
-            word_pools.append(pool_tile)
+            return pool_tile
 
-        scale_pools = []
-        first_row = (96, 96)
-        empty_rows = (((0, 96),), ((0, 96),))
-        for level, (name, scales) in enumerate((("k", k_scales), ("c", c_scales))):
-            pool_tile = keep.tile([P, TOKENS // 4], I32, name=name + "_scale_pool", tag=name + "_first", align_bytes=64)
-            for lo, hi in empty_rows[level]:
-                nc.vector.memset(pool_tile[lo:hi, :], 0)
-            at = first_row[level]
-            nc.sync.dma_start(pool_tile[at : at + 32, :], scales.bitcast(I32).rearrange("o f t -> f o t"))
-            scale_pools.append(pool_tile)
+        def make_planes(name, pool_tile, queues):
+            plane = keep.tile([P, PASSES, SLOTS // 4], I32, name=name + "_planes", align_bytes=64)
+            nc.vector.memset(plane[:], 0)
+            picked = keep.tile([P, SLOTS], U8, name=name + "_picked_scales", align_bytes=64)
+            nc.vector.tensor_copy(picked[:], pool_tile[:].bitcast(U8).indirect(offsets[:]))
+            for quad in range(4):
+                queues[quad % len(queues)].dma_start(
+                    plane[32 * quad : 32 * quad + 4, :, :],
+                    picked[SCALE_ROW + 8 * quad : SCALE_ROW + 8 * quad + 8, :].bitcast(I32),
+                )
+            return plane
 
+        k_scale_pool = load_scales("k", k_scales)
+        c_scale_pool = load_scales("c", c_scales)
+        q_raw = keep.tile([P, PASSES, PACK, QUERIES], F32, name="q_raw", align_bytes=64)
         nc.sync.dma_start(
             q_raw[:].rearrange("p o j w -> p o (j w)"),
             qT[0].rearrange("(o p j) w -> p o (j w)", o=PASSES, j=PACK),
         )
-        load_words("k", k_words, "k_words")
-
-        planes = []
-        for name in ("k", "c"):
-            plane = keep.tile([P, PASSES, SLOTS // 4], I32, name=name + "_planes", align_bytes=64)
-            nc.vector.memset(plane[:], 0)
-            planes.append(plane)
-
-        def pick_scales(level, name, queues):
-            picked = keep.tile([P, SLOTS], U8, name=name + "_picked_scales", align_bytes=64)
-            nc.vector.tensor_copy(picked[:], scale_pools[level][:].bitcast(U8).indirect(offsets[:]))
-            for quad in range(4):
-                queues[quad % len(queues)].dma_start(
-                    planes[level][32 * quad : 32 * quad + 4, :, :],
-                    picked[first_row[level] + 8 * quad : first_row[level] + 8 * quad + 8, :].bitcast(I32),
-                )
-
-        pick_scales(0, "k", [nc.sync, nc.scalar])
-        load_words("c", c_words, "k_first")
-        pick_scales(1, "c", [nc.sync])
-
-        def pick_words(level, name, first, count):
-            picked = keep.tile([P, count], U32, name=name + "_picked", align_bytes=64)
-            nc.vector.tensor_copy(
-                picked[:],
-                word_pools[level][:].bitcast(U32).indirect(offsets[:, first // 16 : (first + count) // 16]),
-            )
-            return picked
-
-        def part_words(picked, name, count, order):
-            parted = keep.tile([P, PASSES, 2 * count], U8, name=name + "_parted", align_bytes=64)
-            halves = picked.bitcast(U16).rearrange("p (n o) -> p o n", o=PASSES)
-            if order is None:
-                nc.vector.tensor_copy(parted[:].bitcast(U16), halves)
-            else:
-                for o in order:
-                    nc.vector.tensor_copy(parted[:, o, :].bitcast(U16), halves[:, o, :])
-            return parted
+        k_word_pool = load_words("k", k_words, "k_words")
+        k_planes = make_planes("k", k_scale_pool, [nc.sync, nc.scalar])
+        c_word_pool = load_words("c", c_words, "k_first")
+        c_planes = make_planes("c", c_scale_pool, [nc.sync])
 
         q_codes = []
         q_scales = []
@@ -107,62 +82,69 @@ def tile_attend_residseg_kernel(tc, qT, k_words, k_scales, c_words, c_scales, of
             q_codes.append(codes)
             q_scales.append(scales)
 
-        half = SLOTS // 2
-        by_pass = {(1, 0): (1, 0), (1, SLOTS - GROUP): (0, 1)}
-        picked_words = []
-        parted_words = []
-        for level, name in enumerate(("k", "c")):
-            halves = [pick_words(level, "%s%d" % (name, h), h * half, half) for h in range(2)]
-            picked_words.append(halves)
-            parted_words.append(
-                [
-                    part_words(halves[at // half][:, at % half : at % half + GROUP], "%s%d" % (name, at), GROUP, by_pass.get((level, at)))
-                    for at in range(0, SLOTS, GROUP)
-                ]
-            )
-
-        scores = [psum.tile([P, GROUP], F32, name="scores%d" % g) for g in range(SLOTS // GROUP)]
-
-        def multiply(level, o, g, first, last):
-            at = g * GROUP
-            nc.tensor.matmul_mx(
-                out=scores[g][:],
-                lhsT=q_codes[o][:].bitcast(FP8X4),
-                lhsT_scale=q_scales[o][:],
-                rhs=parted_words[level][g][:, o, :].bitcast(FP4X4),
-                rhs_scale=planes[level][:, o, :].bitcast(U8)[:, at : at + GROUP],
-                start=first,
-                stop=last,
-            )
-
-        for g in range(SLOTS // GROUP):
-            order = (1, 0) if g % 2 == 0 else (0, 1)
-            for o in order:
-                multiply(0, o, g, o == order[0], False)
-
-        spare = psum.tile([P, SLOTS], F32, name="spare")
-        nc.tensor.matmul_mx(
-            out=spare[:],
-            lhsT=q_codes[1][:].bitcast(FP8X4),
-            lhsT_scale=q_scales[1][:],
-            rhs=picked_words[0][1][:].bitcast(U8).bitcast(FP4X4),
-            rhs_scale=planes[0][:, 1, :].bitcast(U8),
-            start=True,
-            stop=True,
-        )
-
+        scores = [psum.tile([P, GROUP], F32, name="scores%d" % g) for g in range(GROUPS)]
         best = keep.tile([P, SLOTS // SEG], F32, name="best")
         per_group = GROUP // SEG
-        for g in range(SLOTS // GROUP):
-            order = (1, 0) if g % 2 == 0 else (0, 1)
+
+        def pick(name, pool_tile, first, count):
+            picked = keep.tile([P, count], U32, name="%s_picked%d" % (name, first), align_bytes=64)
+            nc.vector.tensor_copy(
+                picked[:], pool_tile[:].bitcast(U32).indirect(offsets[:, first // 16 : (first + count) // 16])
+            )
+            return picked
+
+        def part(name, picked, count, order):
+            parted = keep.tile([P, PASSES, 2 * count], U8, name=name, align_bytes=64)
+            halves = picked.bitcast(U16).rearrange("p (n o) -> p o n", o=PASSES)
+            if order is None:
+                nc.vector.tensor_copy(parted[:].bitcast(U16), halves)
+            else:
+                for o in order:
+                    nc.vector.tensor_copy(parted[:, o, :].bitcast(U16), halves[:, o, :])
+            return parted
+
+        def pass_order(g):
+            return (1, 0) if g % 2 == 0 else (0, 1)
+
+        def multiply(parted, at, plane, g, opens):
+            order = pass_order(g)
             for o in order:
-                multiply(1, o, g, False, o == order[-1])
+                nc.tensor.matmul_mx(
+                    out=scores[g][:],
+                    lhsT=q_codes[o][:].bitcast(FP8X4),
+                    lhsT_scale=q_scales[o][:],
+                    rhs=parted[:, o, 2 * at : 2 * (at + GROUP)].bitcast(FP4X4),
+                    rhs_scale=plane[:, o, :].bitcast(U8)[:, g * GROUP : (g + 1) * GROUP],
+                    start=opens and o == order[0],
+                    stop=not opens and o == order[-1],
+                )
+
+        def reduce(g):
             nc.vector.tensor_reduce(
                 out=best[:, g * per_group : (g + 1) * per_group],
                 in_=scores[g][:].rearrange("p (j s) -> p j s", s=SEG),
                 axis=mybir.AxisListType.X,
                 op=mybir.AluOpType.max,
             )
-            if g in (0, SLOTS // GROUP - 1):
-                done = slice(min(g, 1) * per_group, (g + 1) * per_group)
-                nc.sync.dma_start(out[0][:, done], best[:, done])
+
+        def store(first, last):
+            done = slice(first * per_group, last * per_group)
+            nc.sync.dma_start(out[0][:, done], best[:, done])
+
+        half = SLOTS // 2
+        k_picked = pick("k", k_word_pool, 0, SLOTS)
+        for h in range(2):
+            k_parted = part("k_parted%d" % h, k_picked[:, h * half : (h + 1) * half], half, None)
+            for at in range(0, half, GROUP):
+                multiply(k_parted, at, k_planes, (h * half + at) // GROUP, True)
+        c_picked = [pick("c", c_word_pool, h * half, half) for h in range(2)]
+        for g in range(GROUPS):
+            at = g * GROUP % half
+            order = pass_order(g) if g in (0, GROUPS - 1) else None
+            c_parted = part("c_parted%d" % g, c_picked[g * GROUP // half][:, at : at + GROUP], GROUP, order)
+            multiply(c_parted, 0, c_planes, g, False)
+        reduce(0)
+        store(0, 1)
+        for g in range(1, GROUPS):
+            reduce(g)
+        store(1, GROUPS)

@@ -133,10 +133,9 @@ def tile_attend_residseg_kernel(tc, qT, k_words, k_scales, c_words, c_scales, of
 
         half = SLOTS // 2
         k_picked = pick("k", k_word_pool, 0, SLOTS)
-        for h in range(2):
-            k_parted = part("k_parted%d" % h, k_picked[:, h * half : (h + 1) * half], half, None)
-            for at in range(0, half, GROUP):
-                multiply(k_parted, at, k_planes, (h * half + at) // GROUP, True)
+        k_parted = part("k_parted", k_picked[:], SLOTS, None)
+        for g in range(GROUPS):
+            multiply(k_parted, g * GROUP, k_planes, g, True)
         c_picked = [pick("c", c_word_pool, h * half, half) for h in range(2)]
         for g in range(GROUPS):
             at = g * GROUP % half

@@ -34,20 +34,20 @@ def tile_attend_residseg_kernel(tc, qT, k_words, k_scales, c_words, c_scales, of
         nc.sync.dma_start(offsets[:], offs)
 
         def load_scales(name, scales):
-            pool_tile = keep.tile([P, TOKENS // 4], I32, name=name + "_scale_pool", tag=name + "_first", align_bytes=64)
+            pool_tile = keep.tile([P, TOKENS // 4], I32, name=name + "_scale_pool", tag=name + "_first", align_bytes=256)
             nc.vector.memset(pool_tile[0:SCALE_ROW, :], 0)
             nc.sync.dma_start(pool_tile[SCALE_ROW:P, :], scales.bitcast(I32).rearrange("o f t -> f o t"))
             return pool_tile
 
         def load_words(name, words, tag):
-            pool_tile = keep.tile([P, TOKENS], I32, name=name + "_word_pool", tag=tag, align_bytes=64)
+            pool_tile = keep.tile([P, TOKENS], I32, name=name + "_word_pool", tag=tag, align_bytes=256)
             nc.sync.dma_start(pool_tile[:], words[0].rearrange("p t b -> p (t b)").bitcast(I32))
             return pool_tile
 
         def make_planes(name, pool_tile, queues):
-            plane = keep.tile([P, PASSES, SLOTS // 4], I32, name=name + "_planes", align_bytes=64)
+            plane = keep.tile([P, PASSES, SLOTS // 4], I32, name=name + "_planes", align_bytes=256)
             nc.vector.memset(plane[:], 0)
-            picked = keep.tile([P, SLOTS], U8, name=name + "_picked_scales", align_bytes=64)
+            picked = keep.tile([P, SLOTS], U8, name=name + "_picked_scales", align_bytes=256)
             nc.vector.tensor_copy(picked[:], pool_tile[:].bitcast(U8).indirect(offsets[:]))
             for quad in range(4):
                 queues[quad % len(queues)].dma_start(
@@ -58,7 +58,7 @@ def tile_attend_residseg_kernel(tc, qT, k_words, k_scales, c_words, c_scales, of
 
         k_scale_pool = load_scales("k", k_scales)
         c_scale_pool = load_scales("c", c_scales)
-        q_raw = keep.tile([P, PASSES, PACK, QUERIES], F32, name="q_raw", align_bytes=64)
+        q_raw = keep.tile([P, PASSES, PACK, QUERIES], F32, name="q_raw", align_bytes=256)
         nc.sync.dma_start(
             q_raw[:].rearrange("p o j w -> p o (j w)"),
             qT[0].rearrange("(o p j) w -> p o (j w)", o=PASSES, j=PACK),
@@ -71,13 +71,13 @@ def tile_attend_residseg_kernel(tc, qT, k_words, k_scales, c_words, c_scales, of
         q_codes = []
         q_scales = []
         for o in range(PASSES):
-            rounded = keep.tile([P, QUERIES * PACK], BF16, name="q_bf%d" % o, align_bytes=64)
+            rounded = keep.tile([P, QUERIES * PACK], BF16, name="q_bf%d" % o, align_bytes=256)
             nc.vector.tensor_copy(
                 rounded[:].rearrange("p (c i j) -> p c j i", i=4, j=PACK),
                 q_raw[:, o].rearrange("p j (c i) -> p c j i", i=4),
             )
-            codes = keep.tile([P, QUERIES], U32, name="q_codes%d" % o, align_bytes=64)
-            scales = keep.tile([P, QUERIES], U8, name="q_scales%d" % o, align_bytes=64)
+            codes = keep.tile([P, QUERIES], U32, name="q_codes%d" % o, align_bytes=256)
+            scales = keep.tile([P, QUERIES], U8, name="q_scales%d" % o, align_bytes=256)
             nc.vector.quantize_mx(out=codes[:].bitcast(FP8X4), scales=scales[:], in_=rounded[:])
             q_codes.append(codes)
             q_scales.append(scales)
@@ -87,14 +87,14 @@ def tile_attend_residseg_kernel(tc, qT, k_words, k_scales, c_words, c_scales, of
         per_group = GROUP // SEG
 
         def pick(name, pool_tile, first, count):
-            picked = keep.tile([P, count], U32, name="%s_picked%d" % (name, first), align_bytes=64)
+            picked = keep.tile([P, count], U32, name="%s_picked%d" % (name, first), align_bytes=256)
             nc.vector.tensor_copy(
                 picked[:], pool_tile[:].bitcast(U32).indirect(offsets[:, first // 16 : (first + count) // 16])
             )
             return picked
 
         def part(name, picked, count, order):
-            parted = keep.tile([P, PASSES, 2 * count], U8, name=name, align_bytes=64)
+            parted = keep.tile([P, PASSES, 2 * count], U8, name=name, align_bytes=256)
             halves = picked.bitcast(U16).rearrange("p (n o) -> p o n", o=PASSES)
             if order is None:
                 nc.vector.tensor_copy(parted[:].bitcast(U16), halves)

from contextlib import ExitStack

import concourse.mybir as mybir

F32 = mybir.dt.float32
BF16 = mybir.dt.bfloat16
I32 = mybir.dt.int32
U32 = mybir.dt.uint32
U16 = mybir.dt.uint16
U8 = mybir.dt.uint8
FP8X4 = mybir.dt.float8_e4m3fn_x4
FP4X4 = mybir.dt.float4_e2m1fn_x4

P = 128
PACK = 4
PASSES = 2
TOKENS = 2048
SLOTS = 512
QUERIES = 128
SEG = 16
GROUP = 128
GROUPS = SLOTS // GROUP
SCALE_ROW = 96
FLOPS = 2 * 2 * QUERIES * SLOTS * PASSES * P * PACK


def tile_attend_residseg_kernel(tc, qT, k_words, k_scales, c_words, c_scales, offs, out):
    nc = tc.nc
    with ExitStack() as ctx:
        keep = ctx.enter_context(tc.tile_pool(name="keep", bufs=1))
        psum = ctx.enter_context(tc.psum_pool(name="psum", bufs=1))

        offsets = keep.tile([P, SLOTS // 16], U16, name="offsets")
        nc.sync.dma_start(offsets[:], offs)

        def load_scales(name, scales):
            pool_tile = keep.tile([P, TOKENS // 4], I32, name=name + "_scale_pool", tag=name + "_first", align_bytes=256)
            nc.vector.memset(pool_tile[0:SCALE_ROW, :], 0)
            nc.sync.dma_start(pool_tile[SCALE_ROW:P, :], scales.bitcast(I32).rearrange("o f t -> f o t"))
            return pool_tile

        def load_words(name, words, tag):
            pool_tile = keep.tile([P, TOKENS], I32, name=name + "_word_pool", tag=tag, align_bytes=256)
            nc.sync.dma_start(pool_tile[:], words[0].rearrange("p t b -> p (t b)").bitcast(I32))
            return pool_tile

        def make_planes(name, pool_tile, queues):
            plane = keep.tile([P, PASSES, SLOTS // 4], I32, name=name + "_planes", align_bytes=256)
            nc.vector.memset(plane[:], 0)
            picked = keep.tile([P, SLOTS], U8, name=name + "_picked_scales", align_bytes=256)
            nc.vector.tensor_copy(picked[:], pool_tile[:].bitcast(U8).indirect(offsets[:]))
            for quad in range(4):
                queues[quad % len(queues)].dma_start(
                    plane[32 * quad : 32 * quad + 4, :, :],
                    picked[SCALE_ROW + 8 * quad : SCALE_ROW + 8 * quad + 8, :].bitcast(I32),
                )
            return plane

        k_scale_pool = load_scales("k", k_scales)
        c_scale_pool = load_scales("c", c_scales)
        q_raw = keep.tile([P, PASSES, PACK, QUERIES], F32, name="q_raw", align_bytes=256)
        nc.sync.dma_start(
            q_raw[:].rearrange("p o j w -> p o (j w)"),
            qT[0].rearrange("(o p j) w -> p o (j w)", o=PASSES, j=PACK),
        )
        k_word_pool = load_words("k", k_words, "k_words")
        k_planes = make_planes("k", k_scale_pool, [nc.sync, nc.scalar])
        c_word_pool = load_words("c", c_words, "k_first")
        c_planes = make_planes("c", c_scale_pool, [nc.sync])

        q_codes = []
        q_scales = []
        for o in range(PASSES):
            rounded = keep.tile([P, QUERIES * PACK], BF16, name="q_bf%d" % o, align_bytes=256)
            nc.vector.tensor_copy(
                rounded[:].rearrange("p (c i j) -> p c j i", i=4, j=PACK),
                q_raw[:, o].rearrange("p j (c i) -> p c j i", i=4),
            )
            codes = keep.tile([P, QUERIES], U32, name="q_codes%d" % o, align_bytes=256)
            scales = keep.tile([P, QUERIES], U8, name="q_scales%d" % o, align_bytes=256)
            nc.vector.quantize_mx(out=codes[:].bitcast(FP8X4), scales=scales[:], in_=rounded[:])
            q_codes.append(codes)
            q_scales.append(scales)

        scores = [psum.tile([P, GROUP], F32, name="scores%d" % g) for g in range(GROUPS)]
        best = keep.tile([P, SLOTS // SEG], F32, name="best")
        per_group = GROUP // SEG

        def pick(name, pool_tile, first, count):
            picked = keep.tile([P, count], U32, name="%s_picked%d" % (name, first), align_bytes=256)
            nc.vector.tensor_copy(
                picked[:], pool_tile[:].bitcast(U32).indirect(offsets[:, first // 16 : (first + count) // 16])
            )
            return picked

        def part(name, picked, count, order):
            parted = keep.tile([P, PASSES, 2 * count], U8, name=name, align_bytes=256)
            halves = picked.bitcast(U16).rearrange("p (n o) -> p o n", o=PASSES)
            if order is None:
                nc.vector.tensor_copy(parted[:].bitcast(U16), halves)
            else:
                for o in order:
                    nc.vector.tensor_copy(parted[:, o, :].bitcast(U16), halves[:, o, :])
            return parted

        def pass_order(g):
            return (1, 0) if g % 2 == 0 else (0, 1)

        def multiply(parted, at, plane, g, opens):
            order = pass_order(g)
            for o in order:
                nc.tensor.matmul_mx(
                    out=scores[g][:],
                    lhsT=q_codes[o][:].bitcast(FP8X4),
                    lhsT_scale=q_scales[o][:],
                    rhs=parted[:, o, 2 * at : 2 * (at + GROUP)].bitcast(FP4X4),
                    rhs_scale=plane[:, o, :].bitcast(U8)[:, g * GROUP : (g + 1) * GROUP],
                    start=opens and o == order[0],
                    stop=not opens and o == order[-1],
                )

        def reduce(g):
            nc.vector.tensor_reduce(
                out=best[:, g * per_group : (g + 1) * per_group],
                in_=scores[g][:].rearrange("p (j s) -> p j s", s=SEG),
                axis=mybir.AxisListType.X,
                op=mybir.AluOpType.max,
            )

        def store(first, last):
            done = slice(first * per_group, last * per_group)
            nc.sync.dma_start(out[0][:, done], best[:, done])

        half = SLOTS // 2
        k_picked = pick("k", k_word_pool, 0, SLOTS)
        k_parted = part("k_parted", k_picked[:], SLOTS, None)
        for g in range(GROUPS):
            multiply(k_parted, g * GROUP, k_planes, g, True)
        c_picked = [pick("c", c_word_pool, h * half, half) for h in range(2)]
        for g in range(GROUPS):
            at = g * GROUP % half
            order = pass_order(g) if g in (0, GROUPS - 1) else None
            c_parted = part("c_parted%d" % g, c_picked[g * GROUP // half][:, at : at + GROUP], GROUP, order)
            multiply(c_parted, 0, c_planes, g, False)
        reduce(0)
        store(0, 1)
        for g in range(1, GROUPS):
            reduce(g)
        store(1, GROUPS)
